import numpy as np
import ml_dtypes


def mxq(x, axis, fmt="e4m3"):
    dtype, down = {"e4m3": (ml_dtypes.float8_e4m3fn, 7), "e5m2": (ml_dtypes.float8_e5m2, 14)}[fmt]
    v = np.moveaxis(np.asarray(x, np.float32).astype(ml_dtypes.bfloat16).astype(np.float64), axis, -1)
    blocks = v.reshape(v.shape[:-1] + (-1, 32))
    amax = np.abs(blocks).max(-1, keepdims=True)
    byte = np.maximum(np.where(amax > 0, np.frexp(amax)[1] - 1 + 127, 0) - down, 1)
    scale = np.exp2(byte - 127.0)
    codes = (blocks / scale).astype(np.float32).astype(dtype).astype(np.float64)
    return np.moveaxis((codes * scale).reshape(v.shape), -1, axis)


WIDE = False


def mx_kscale(k):
    if not WIDE:
        return np.ones(k)
    levels = np.array([10, -10, 5, -5, 0])
    if k % 512:
        return np.exp2(np.random.permutation(np.resize(levels, k // 32))).repeat(32)
    a = np.empty((k // 512, 16))
    for p in range(k // 512):
        a[p, :8] = np.random.permutation(np.resize(levels, 8))
        for g in range(8):
            far = levels[np.abs(levels - a[p, g]) >= 10]
            a[p, g + 8] = far[np.random.randint(len(far))]
    return np.exp2(a.ravel()).repeat(32)


BF16 = ml_dtypes.bfloat16


def bf(x):
    return np.asarray(x, np.float32).astype(BF16)


def f64(x):
    return np.asarray(x).astype(np.float64)


V, R, D, T, S = 2048, 512, 1024, 512, 512

CAP = 5.0
EMB_SCALE = 8.0


def rms_rows(z):
    return z / np.sqrt(np.mean(np.square(z), axis=1, keepdims=True))


def draw0():
    s, t, u = mx_kscale(R), mx_kscale(D), mx_kscale(V)
    size = np.exp(0.4 * np.random.standard_normal((V, 1)))
    codes = np.random.standard_normal((V, R)) * size
    basis = np.random.standard_normal((R, D)) / np.sqrt(R)
    hidden = 2.0 * np.random.standard_normal((T, D)) / np.sqrt(D)
    mix = np.exp(1.5 * np.random.standard_normal((S, V)))
    mix = mix / mix.sum(axis=1, keepdims=True)
    return {"codes": bf(codes * s),
            "basis": bf(basis / s[:, None]),
            "basis_bias": bf(0.1 * np.random.standard_normal(D)),
            "feat_gain": bf((1 + 0.1 * np.random.standard_normal(D)) * t),
            "word_gain": bf((1 + 0.1 * np.random.standard_normal(V)) * u),
            "hidden": bf(hidden / t),
            "out_scale": bf((1 + 0.1 * np.random.standard_normal(V)) / u),
            "out_bias": bf(0.3 * np.random.standard_normal(V)),
            "mix": bf(mix / u),
            "in_gain": bf((1 + 0.1 * np.random.standard_normal(D)) / t),
            "pos": bf(0.3 * np.random.standard_normal((S, D)))}


def core(codes, basis, basis_bias, feat_gain, word_gain, hidden, out_scale, out_bias, mix, in_gain, pos):
    z = (mxq(f64(codes), 1, "e4m3") @ mxq(f64(basis), 0, "e4m3")) + f64(basis_bias)[None, :]
    e = rms_rows(z) * f64(feat_gain)[None, :] * f64(word_gain)[:, None]
    l = mxq(f64(hidden), 1, "e4m3") @ mxq(e, 1, "e4m3").T
    l = l * f64(out_scale)[None, :] + f64(out_bias)[None, :]
    logits = CAP * np.tanh(l / CAP)
    x = mxq(f64(mix), 1, "e4m3") @ mxq(e, 0, "e4m3")
    embedded = EMB_SCALE * x * f64(in_gain)[None, :] + f64(pos)
    return logits, embedded


def e4m3fn_bytes(y):
    return np.clip(np.asarray(y, np.float64), -448.0, 448.0).astype(np.float32).astype(ml_dtypes.float8_e4m3fn).view(np.uint8)


def e4m3fn_values(b):
    return np.asarray(b, np.uint8).view(ml_dtypes.float8_e4m3fn).astype(np.float64)


def setup_inputs():
    d = draw0()
    x0 = np.asarray(d['mix']).astype(np.float64)
    s = (np.max(np.abs(x0), axis=(0,), keepdims=True) / 448.0).astype(np.float32)
    out = {}
    for k, v in d.items():
        if k == 'mix':
            out['mix_bytes'] = e4m3fn_bytes(x0 / s.astype(np.float64))
            out['mix_scale'] = s
        else:
            out[k] = v
    return out


def reference(codes, basis, basis_bias, feat_gain, word_gain, hidden, out_scale, out_bias, mix_bytes, mix_scale, in_gain, pos):
    return core(codes, basis, basis_bias, feat_gain, word_gain, hidden, out_scale, out_bias, e4m3fn_values(mix_bytes) * mix_scale.astype(np.float64), in_gain, pos)

from contextlib import ExitStack

import concourse.mybir as mybir
from concourse.masks import make_identity

V, R, D, T, S = 2048, 512, 1024, 512, 512
FLOPS = 2 * V * R * D + 2 * T * V * D + 2 * S * V * D

F32 = mybir.dt.float32
BF16 = mybir.dt.bfloat16
U32 = mybir.dt.uint32
U8 = mybir.dt.uint8
FP8 = mybir.dt.float8_e4m3fn
X4 = mybir.dt.float8_e4m3fn_x4
ACT = mybir.ActivationFunctionType
ALU = mybir.AluOpType

P = 128
PACK = 4
K_PASS = P * PACK
BANK = 512
GROUPS = V // K_PASS
TILES = V // P
HALVES = D // BANK
BLOCKS = 4
CAP = 5.0
EMB_SCALE = 8.0

PSUM_BUFS = {"z": 3, "turned": 2, "back": 2, "logits": 1}
EMBED_IN_TURNED = (3, 4)
EMBED_ADD_ON_GPSIMD = 4

ORDER = """
weave_basis 0 0, spread 0, weave_basis 0 1, weave_basis 1 0, quantise_basis 0, turn_codes 0 0, take_codes 0 0,
quantise_first_codes 0, turn_codes 0 1, weave_basis 1 1, product 0 0, take_codes 0 1, quantise_basis 1,
quantise_first_codes 1, product 0 1, bias 0 0, bias 0 1, gain_constants, product 1 0, squares 0, product 2 0,
bias 1 0, norm 0, bias 2 0, spread 1, weigh 0, product 1 1, bias 1 1, product 2 1, bias 2 1, turn_codes 1 0,
squares 1, cap_constants, product 3 0, bias 3 0, take_codes 1 0, norm 1, product 3 1, turn_codes 1 1, turn_hidden 0,
turn_hidden 3, scale 0, take_hidden 0, take_codes 1 1, turn_codes 2 0, take_hidden 3, turn_hidden 2, bias 3 1,
widen_mix 0 0, turn_codes 2 1, quantise_codes 1, product 4 0, product 4 1, weigh 1, scale 1, widen_mix 0 1,
product 5 0, take_codes 2 0, squares 2, squares 3, take_hidden 2, norm 2, norm 3, take_codes 2 1, weigh 2, bias 4 0,
bias 4 1, turn_hidden 1, take_hidden 1, weigh 3, turn_table 0, take_table 0, turn_table 1, product 6 0, bias 5 0,
take_table 1, squares 4, scale 2, product 5 1, scale 3, turn_mix 0 0, take_mix 0 0, quantise_table 0, turn_table 2,
take_table 2, product 6 1, bias 5 1, squares 5, weave_words 0 0, turn_table 3, take_table 3, take_words 0 0,
bias 6 0, norm 4, weigh 4, norm 5, quantise_hidden, quantise_table 1, bias 6 1, product 7 0, bias 7 0,
weave_words 0 1, squares 6, norm 6, logits 0, cap 0, widen_mix 0 2, quantise_table 2, quantise_table 3, scale 4,
turn_codes 3 0, take_codes 3 0, take_words 0 1, product 7 1, weave_words 0 2, take_words 0 2, weigh 5, logits 2,
turn_mix 1 0, cap 2, take_mix 1 0, weigh 6, quantise_codes 2, bias 7 1, weave_words 0 3, turn_table 4, product 8 0,
logits 1, squares 7, scale 5, turn_table 5, take_words 0 3, scale 6, norm 7, product 8 1, cap 1, take_table 4,
weigh 7, take_table 5, bias 8 0, bias 8 1, widen_mix 0 3, quantise_table 4, squares 8, logits 3, product 9 1, cap 3,
turn_codes 3 1, take_codes 3 1, product 9 0, product 10 0, bias 9 0, bias 10 0, norm 8, weigh 8, turn_table 6,
take_table 6, turn_logits 0 2, store_logits 0 2, logits 4, turn_logits 0 3, cap 4, bias 9 1, squares 9,
store_logits 0 3, quantise_table 5, product 11 0, scale 7, product 10 1, turn_mix 0 1, weave_words 1 0,
take_words 1 0, product 11 1, weave_words 1 2, turn_logits 0 1, turn_table 7, bias 10 1, quantise_table 6, scale 8,
quantise_codes 3, logits 6, product 12 1, turn_mix 1 1, norm 9, take_mix@vector 0 1, squares 10, norm 10,
take_words 1 2, take_table 7, weigh 9, cap 6, bias 11 0, bias 11 1, weigh 10, squares 11, take_mix 1 1, logits 5,
product 12 0, turn_table 8, cap 5, quantise_words 0 0 2, quantise_table 7, turn_logits 0 0, store_logits 0 1,
norm 11, weigh 11, take_table 8, product 13 0, logits 7, scale 9, cap 7, bias 12 0, bias 12 1, turn_table 9,
scale 10, store_logits 0 0, quantise_table 8, turn_logits 1 0, product 13 1, take_table 9, store_logits 1 0,
product 14 0, weave_words 1 1, logits 8, turn_logits 1 2, squares 12, norm 12, turn_table 10, take_words 1 1,
widen_mix 1 0, scale 11, turn_table 11, store_logits 1 2, turn_logits 1 3, weave_words 1 3, cap 8, take_table 10,
store_logits 1 3, weigh 12, take_table 11, take_words 1 3, quantise_table 9, quantise_mix 0, bias 13 0, bias 13 1,
product 15 0, logits 9, widen_mix 1 1, cap 9, weave_words 2 0, take_words 2 0, widen_mix 1 2, quantise_table 10,
squares 13, product 14 1, quantise_table 11, widen_mix 1 3, weave_words 2 2, turn_mix 2 0, turn_logits 1 1,
logits 10, bias 14 0, bias 14 1, turn_mix 2 1, take_mix 2 0, bias 15 0, take_words 2 2, store_logits 1 1, cap 10,
take_mix 2 1, norm 13, squares 14, turn_mix 3 0, norm 14, weave_words 2 1, product 15 1, take_words 2 1,
weave_words 2 3, take_words 2 3, take_mix 3 0, weigh 13, quantise_words 1 0 2, quantise_mix 1, embed 0 0 2,
embed 1 0 2, logits 11, scale 12, turn_table 12, turn_mix 3 1, cap 11, turn_logits 2 0, quantise_mix 2, bias 15 1,
squares 15, weigh 14, take_table 12, quantise_words 2 0 2, embed 2 0 3, store_logits 2 0, scale 13, embed 1 2 3,
turn_logits 2 1, norm 15, weigh 15, turn_table 13, take_mix@vector 3 1, store_logits 2 1, turn_logits 2 3,
take_table 13, quantise_table 12, logits 12, turn_logits 2 2, scale 14, turn_table 14, store_logits 2 3,
embed 0 2 3, scale 15, cap 12, store_logits 2 2, take_table 14, quantise_table 13, weave_words 3 3, take_words 3 3,
copy_words 3 0, copy_words 3 1, quantise_table 14, quantise_mix 3, quantise_words 3 0 1, logits 13, cap 13,
turn_table 15, take_table 15, weave_words 3 2, quantise_table 15, logits 14, take_words 3 2, quantise_words 3 1 2,
embed 4 0 3, embed 2 3 4, embed 0 3 4, gain 2, store_embed 2, embed 1 3 4, gain 1, store_embed 1, gain 0, cap 14,
logits 15, embed 3 0 3, embed 4 3 4, cap 15, turn_logits 3 1, store_logits 3 1, turn_logits 3 3, gain 4,
store_embed 4, embed 5 0 4, embed 3 3 4, store_logits 3 3, turn_logits 3 0, turn_logits 3 2, store_logits 3 0,
store_logits 3 2, gain 5, gain 3, embed 7 0 4, store_embed 0, store_embed 5, gain 7, embed 6 0 4, gain 6,
store_embed 3, store_embed 7, store_embed 6
"""


def tile_tied_factorised_embedding_f6_kernel(
    tc, codes, basis, basis_bias, feat_gain, word_gain, hidden, out_scale, out_bias,
    mix_bytes, mix_scale, in_gain, pos, out_0, out_1,
):
    nc = tc.nc
    with ExitStack() as ctx:
        keep = ctx.enter_context(tc.tile_pool(name="keep", bufs=1))
        work = ctx.enter_context(tc.tile_pool(name="work", bufs=3))
        psum = ctx.enter_context(tc.psum_pool(name="psum", bufs=1))

        def bank(tag):
            return psum.tile([P, BANK], F32, name=tag, tag=tag, bufs=PSUM_BUFS[tag])

        rows = []
        for i, vec in enumerate((basis_bias, feat_gain)):
            row = work.tile([P, D], BF16, name=f"row{i}", tag="unread", bufs=2)
            nc.vector.memset(row[:], 0.0)
            nc.sync.dma_start(out=row[0:1, :], in_=vec.rearrange("(o d) -> o d", o=1))
            rows.append(row)
        ones = keep.tile([P, P], BF16, name="ones")
        nc.vector.memset(ones[:], 1.0)
        first_in = keep.tile([P, 1], F32, name="first_in")
        nc.vector.memset(first_in[:], 0.0)
        first_out = keep.tile([P, 1], F32, name="first_out")
        nc.scalar.activation(out=first_out[:], in_=first_in[:], func=ACT.Tanh)
        minus_half = keep.tile([P, 1], F32, name="minus_half")
        nc.vector.memset(minus_half[:], -0.5)
        ident = keep.tile([P, P], F32, name="ident")
        make_identity(nc, ident[:])
        ident_b = keep.tile([P, P], BF16, name="ident_b")
        nc.vector.tensor_copy(out=ident_b[:], in_=ident[:])

        basis_rows = keep.tile([P, HALVES, PACK, BANK], BF16, name="basis_rows")
        code_rows = []
        for g in range(GROUPS):
            rows_g = keep.tile([P, PACK, R], BF16, name=f"code_rows{g}")
            code_rows.append(rows_g)
        hidden_rows = keep.tile([P, BLOCKS, D], BF16, name="hidden_rows")
        mix_codes = keep.tile([P, BLOCKS, V], U8, name="mix_codes")
        mix_scales = keep.tile([P, V], F32, name="mix_scales")
        pos_rows = keep.tile([P, BLOCKS, D], BF16, name="pos_rows")
        gains = keep.tile([P, 3 * D], BF16, name="gains")
        bias_b, feat_b, in_b = gains[:, 0:D], gains[:, D : 2 * D], gains[:, 2 * D : 3 * D]

        def load_basis(h):
            nc.sync.dma_start(
                out=basis_rows[:, h], in_=basis.rearrange("(p j) d -> p j d", j=PACK)[:, :, h * BANK : (h + 1) * BANK]
            )

        def load_codes(g, t0, t1):
            nc.sync.dma_start(
                out=code_rows[g][:, t0:t1, :],
                in_=codes[g * K_PASS : (g + 1) * K_PASS, :].rearrange("(m t) r -> m t r", t=PACK)[:, t0:t1, :],
            )

        load_basis(0)
        load_codes(0, 0, 2)
        load_basis(1)
        load_codes(0, 2, 4)
        nc.sync.dma_start(out=hidden_rows[:], in_=hidden.rearrange("(a p) d -> p a d", p=P))
        load_codes(1, 0, 4)
        per_word = []
        for name, vec in (("word_gains", word_gain), ("out_scales", out_scale), ("out_biases", out_bias)):
            column = keep.tile([P, GROUPS, PACK], BF16, name=name)
            nc.gpsimd.dma_start(out=column[:], in_=vec.rearrange("(g m t) -> m g t", m=P, t=PACK))
            per_word.append(column)
        word_gains, out_scales, out_biases = per_word
        nc.sync.dma_start(out=mix_codes[:], in_=mix_bytes.rearrange("(a p) k -> p a k", p=P))
        nc.sync.dma_start(out=mix_scales[:], in_=mix_scale.rearrange("o k -> (o k)").partition_broadcast(P))
        load_codes(2, 0, 4)
        load_codes(3, 0, 4)
        nc.sync.dma_start(out=pos_rows[:], in_=pos.rearrange("(a p) d -> p a d", p=P))
        nc.sync.dma_start(out=in_b, in_=in_gain.partition_broadcast(P))

        def operand(pool, name, width, bufs):
            packed = pool.tile([P, width], U32, name=name + "_packed", bufs=bufs, align_bytes=64)
            scales = pool.tile([P, width], U8, name=name + "_scales", bufs=bufs, align_bytes=64)
            return packed, scales

        def quantise(op, lo, hi, src):
            nc.vector.quantize_mx(out=op[0][:, lo:hi].bitcast(X4), scales=op[1][:, lo:hi], in_=src)

        def matmul(out, left, l0, right, r0, start, stop):
            nc.tensor.matmul_mx(
                out=out,
                lhsT=left[0][:, l0 : l0 + P].bitcast(X4),
                lhsT_scale=left[1][:, l0 : l0 + P],
                rhs=right[0][:, r0 : r0 + BANK].bitcast(X4),
                rhs_scale=right[1][:, r0 : r0 + BANK],
                start=start,
                stop=stop,
            )

        basis_q = operand(keep, "basis_q", D, 1)
        codes_q = [operand(keep, f"codes_q{g}", PACK * P, 1) for g in range(GROUPS)]
        hidden_q = operand(keep, "hidden_q", HALVES * T, 1)
        mix_q = [operand(keep, f"mix_q{g}", S, 1) for g in range(GROUPS)]
        words_q = [operand(keep, f"words_q{g}", D, 1) for g in range(GROUPS)]

        def interleave(on_vector, dst, src):
            to = dst.rearrange("p (c i t) -> p c t i", i=4, t=PACK)
            frm = src.rearrange("p t (c i) -> p c t i", i=4)
            if on_vector:
                nc.vector.tensor_copy(out=to, in_=frm)
            else:
                nc.scalar.copy(to, frm)

        def turn_words(out, words, first):
            for u in range(2):
                nc.tensor.transpose(
                    out[:, u * P : (u + 1) * P], words[:, first + u : first + 2 * P : 2], ident[:]
                )

        def move_words(dst, src, on_vector):
            if on_vector:
                nc.vector.tensor_copy(out=dst, in_=src)
            else:
                nc.scalar.copy(dst, src)

        turned = {}

        basis_side = work.tile([P, D * PACK], BF16, name="basis_side", tag="side", bufs=2, align_bytes=64)
        hidden_side = work.tile([P, HALVES * T * PACK], BF16, name="hidden_side", tag="side", bufs=2, align_bytes=64)

        def spread(i):
            for h in range(HALVES):
                b = bank("z" if i == 0 else "back")
                cols = slice(h * BANK, (h + 1) * BANK)
                nc.tensor.matmul(b[:], lhsT=ones[:], rhs=rows[i][:, cols], start=True, stop=True)
                nc.scalar.copy(gains[:, i * D + h * BANK : i * D + (h + 1) * BANK], b[:])

        def weave_basis(h, i):
            c0 = h * BANK + i * (BANK // 2)
            interleave(
                i == 0,
                basis_side[:, PACK * c0 : PACK * (c0 + BANK // 2)],
                basis_rows[:, h, :, i * (BANK // 2) : (i + 1) * (BANK // 2)],
            )

        def quantise_basis(h):
            quantise(basis_q, h * BANK, (h + 1) * BANK, basis_side[:, h * PACK * BANK : (h + 1) * PACK * BANK])

        scale_cap = keep.tile([P, TILES], F32, name="scale_cap")
        bias_cap = keep.tile([P, TILES], F32, name="bias_cap")

        def cap_constants():
            for dst, src in ((scale_cap, out_scales), (bias_cap, out_biases)):
                nc.vector.tensor_scalar(
                    out=dst[:], in0=src[:].rearrange("p g t -> p (g t)"), scalar1=1.0 / CAP, scalar2=None, op0=ALU.mult
                )

        code_side = {}

        def turn_codes(g, i):
            b = bank("turned")
            for k in range(2):
                turn_words(b[:, 2 * k * P : 2 * (k + 1) * P], code_rows[g][:, 2 * i + k, :].bitcast(F32), 0)
            turned["codes", g, i] = b

        def take_codes(g, i, on_vector):
            if g not in code_side:
                side = work.tile([P, PACK * P * PACK], BF16, name="code_side", bufs=2, align_bytes=64)
                code_side[g] = side
            half = code_side[g][:, i * 2 * P * PACK : (i + 1) * 2 * P * PACK]
            move_words(
                half.bitcast(F32).rearrange("p (k m u) -> p k m u", k=2, u=2),
                turned["codes", g, i][:].rearrange("p (k u m) -> p k m u", k=2, u=2),
                on_vector,
            )

        def quantise_codes(g):
            quantise(codes_q[g], 0, PACK * P, code_side[g][:])

        def quantise_first_codes(i):
            w = 2 * P
            quantise(codes_q[0], i * w, (i + 1) * w, code_side[0][:, i * w * PACK : (i + 1) * w * PACK])

        def turn_hidden(a):
            b = bank("back")
            for h in range(HALVES):
                turn_words(b[:, 2 * h * P : 2 * (h + 1) * P], hidden_rows[:, a, :].bitcast(F32), h * 2 * P)
            turned["hidden", a] = b

        def take_hidden(a, on_vector):
            dst = hidden_side[:].bitcast(F32).rearrange("p (h i u) -> p h i u", h=HALVES, u=2)
            move_words(
                dst[:, :, a * P : (a + 1) * P, :],
                turned["hidden", a][:].rearrange("p (h u i) -> p h i u", h=HALVES, u=2),
                on_vector,
            )

        def quantise_hidden():
            quantise(hidden_q, 0, HALVES * T, hidden_side[:])

        mix_wide, mix_side = {}, {}

        def widen_mix(pair, a):
            if pair not in mix_wide:
                wide = work.tile([P, BLOCKS, 2 * K_PASS], BF16, name="mix_wide", bufs=2)
                mix_wide[pair] = wide
            cols = slice(pair * 2 * K_PASS, (pair + 1) * 2 * K_PASS)
            nc.vector.tensor_tensor(
                out=mix_wide[pair][:, a, :], in0=mix_codes[:, a, cols].bitcast(FP8), in1=mix_scales[:, cols], op=ALU.mult
            )

        def turn_mix(g, i):
            b = bank("turned")
            for k in range(2):
                words = mix_wide[g // 2][:, 2 * i + k, :].bitcast(F32)
                turn_words(b[:, 2 * k * P : 2 * (k + 1) * P], words, (g % 2) * 2 * P)
            turned["mix", g, i] = b

        def take_mix(g, i, on_vector):
            if g not in mix_side:
                side = work.tile([P, S * PACK], BF16, name="mix_side", bufs=2, align_bytes=64)
                mix_side[g] = side
            half = mix_side[g][:, i * 2 * P * PACK : (i + 1) * 2 * P * PACK]
            move_words(
                half.bitcast(F32).rearrange("p (k s u) -> p k s u", k=2, u=2),
                turned["mix", g, i][:].rearrange("p (k u s) -> p k s u", k=2, u=2),
                on_vector,
            )

        def quantise_mix(g):
            quantise(mix_q[g], 0, S, mix_side[g][:])

        z, biased, sums, inverses, weights, table = {}, {}, {}, {}, {}, {}

        def product(n, h):
            g, t = divmod(n, PACK)
            b = bank("z")
            matmul(b[:], codes_q[g], t * P, basis_q, h * BANK, True, True)
            z[n, h] = b

        def bias(n, h):
            if n not in biased:
                b = work.tile([P, D], F32, name="biased", bufs=4)
                biased[n] = b
            cols = slice(h * BANK, (h + 1) * BANK)
            nc.vector.tensor_tensor(out=biased[n][:, cols], in0=z[n, h][:], in1=bias_b[:, cols], op=ALU.add)

        def squares(n):
            unread = work.tile([P, D], BF16, name="unread", tag="unread", bufs=2)
            total = work.tile([P, 1], F32, name="total", bufs=3)
            sums[n] = total
            nc.scalar.activation(
                out=unread[:], in_=biased[n][:], func=ACT.Square, scale=1.0 / 32.0, accum_out=total[:]
            )

        word_gains32 = keep.tile([P, TILES], F32, name="word_gains32")

        def gain_constants():
            nc.vector.tensor_copy(out=word_gains32[:], in_=word_gains[:].rearrange("p g t -> p (g t)"))

        def norm(n):
            inverse = work.tile([P, 1], F32, name="inverse", bufs=3)
            nc.gpsimd.tensor_tensor(out=inverse[:], in0=sums[n][:], in1=minus_half[:], op=ALU.pow)
            inverses[n] = inverse

        def weigh(n):
            weight = work.tile([P, 1], F32, name="weight", bufs=3)
            nc.scalar.activation(
                out=weight[:], in_=inverses[n][:], func=ACT.Copy, scale=word_gains32[:, n : n + 1]
            )
            weights[n] = weight

        def scale(n):
            g, t = divmod(n, PACK)
            if g not in table:
                tiles = work.tile([P, PACK, D], BF16, name="table", bufs=2)
                table[g] = tiles
            nc.vector.scalar_tensor_tensor(
                out=table[g][:, t, :], in0=biased[n][:], scalar=weights[n][:], in1=feat_b, op0=ALU.mult, op1=ALU.mult
            )

        feature_side, feature_q, logit, capped = {}, {}, {}, {}

        def turn_table(n):
            g, t = divmod(n, PACK)
            b = bank("turned")
            for h in range(HALVES):
                turn_words(b[:, 2 * h * P : 2 * (h + 1) * P], table[g][:, t, :].bitcast(F32), h * 2 * P)
            turned["table", n] = b

        def take_table(n, on_vector):
            side = work.tile([P, D], BF16, name="feature_side", bufs=3, align_bytes=64)
            feature_side[n] = side
            move_words(
                side[:].bitcast(F32).rearrange("p (h v u) -> p h v u", h=HALVES, u=2),
                turned["table", n][:].rearrange("p (h u v) -> p h v u", h=HALVES, u=2),
                on_vector,
            )

        def quantise_table(n):
            feature_q[n] = operand(work, "feature_q", HALVES * P, 3)
            quantise(feature_q[n], 0, HALVES * P, feature_side[n][:])

        def logits(n):
            b = bank("logits")
            logit[n] = b
            for h in range(HALVES):
                matmul(b[:], feature_q[n], h * P, hidden_q, h * T, h == 0, h == HALVES - 1)

        def cap(n):
            c = work.tile([P, T], F32, name="capped", tag="capped", bufs=9)
            capped[n] = c
            nc.scalar.activation(
                out=c[:], in_=logit[n][:], func=ACT.Tanh, bias=bias_cap[:, n : n + 1], scale=scale_cap[:, n : n + 1]
            )

        def turn_logits(g, a):
            b = bank("back")
            for t in range(PACK):
                nc.tensor.transpose(
                    b[:, t * P : (t + 1) * P], capped[PACK * g + t][:, a * P : (a + 1) * P], ident[:]
                )
            turned["logits", g, a] = b

        def store_logits(g, a, on_vector):
            o = work.tile([P, K_PASS], F32, name="logit_rows", bufs=4)
            dst = o[:].rearrange("p (m t) -> p m t", t=PACK)
            src = turned["logits", g, a][:].rearrange("p (t m) -> p m t", t=PACK)
            if on_vector:
                nc.vector.tensor_scalar(out=dst, in0=src, scalar1=CAP, scalar2=None, op0=ALU.mult)
            else:
                nc.scalar.mul(dst, src, CAP)
            nc.sync.dma_start(out=out_0[a * P : (a + 1) * P, g * K_PASS : (g + 1) * K_PASS], in_=o[:])

        word_side = {}
        quarter = D // 4

        def side_of(g):
            if g not in word_side:
                side = work.tile([P, PACK * D], BF16, name="word_side", tag="side", bufs=2, align_bytes=64)
                word_side[g] = side
            return word_side[g]

        def weave_words(g, q):
            b = psum.tile([P, PACK * quarter], BF16, name="woven", tag="back", bufs=PSUM_BUFS["back"])
            turned["words", g, q] = b
            src = table[g][:].rearrange("p t d -> p d t")
            for i in range(2):
                d0 = q * quarter + i * P
                nc.tensor.matmul(
                    b[:, i * BANK : (i + 1) * BANK], lhsT=ident_b[:], rhs=src[:, d0 : d0 + P, :], start=True, stop=True
                )

        def take_words(g, q):
            nc.scalar.copy(
                side_of(g)[:, q * PACK * quarter : (q + 1) * PACK * quarter], turned["words", g, q][:]
            )

        def copy_words(g, q):
            interleave(
                True,
                side_of(g)[:, q * PACK * quarter : (q + 1) * PACK * quarter],
                table[g][:, :, q * quarter : (q + 1) * quarter],
            )

        def quantise_words(g, h0, h1):
            quantise(words_q[g], h0 * BANK, h1 * BANK, word_side[g][:, h0 * PACK * BANK : h1 * PACK * BANK])

        embedding, embed_rows = {}, {}

        def embed(j, g0, g1):
            h, a = divmod(j, BLOCKS)
            if g0 == 0:
                b = bank("turned" if j in EMBED_IN_TURNED else "z")
                embedding[j] = b
            for g in range(g0, g1):
                matmul(embedding[j][:], mix_q[g], a * P, words_q[g], h * BANK, g == 0, g == GROUPS - 1)

        def gain(j):
            h = j // BLOCKS
            o = work.tile([P, BANK], F32, name="embed_rows", tag="capped", bufs=9)
            embed_rows[j] = o
            nc.vector.scalar_tensor_tensor(
                out=o[:], in0=embedding[j][:], scalar=EMB_SCALE, in1=in_b[:, h * BANK : (h + 1) * BANK],
                op0=ALU.mult, op1=ALU.mult,
            )

        def store_embed(j):
            h, a = divmod(j, BLOCKS)
            cols = slice(h * BANK, (h + 1) * BANK)
            o = embed_rows[j]
            engine = nc.gpsimd if j < EMBED_ADD_ON_GPSIMD else nc.vector
            engine.tensor_tensor(out=o[:], in0=o[:], in1=pos_rows[:, a, cols], op=ALU.add)
            nc.sync.dma_start(out=out_1[a * P : (a + 1) * P, cols], in_=o[:])

        either_engine = {
            "take_codes": take_codes, "take_hidden": take_hidden, "take_mix": take_mix, "take_table": take_table,
            "store_logits": store_logits,
        }
        one_engine = {
            "spread": spread, "weave_basis": weave_basis, "quantise_basis": quantise_basis,
            "cap_constants": cap_constants, "turn_codes": turn_codes, "quantise_codes": quantise_codes,
            "quantise_first_codes": quantise_first_codes, "turn_hidden": turn_hidden,
            "quantise_hidden": quantise_hidden, "widen_mix": widen_mix, "turn_mix": turn_mix,
            "quantise_mix": quantise_mix, "product": product, "bias": bias, "squares": squares,
            "gain_constants": gain_constants, "norm": norm, "weigh": weigh, "scale": scale, "turn_table": turn_table, "quantise_table": quantise_table, "logits": logits, "cap": cap,
            "turn_logits": turn_logits, "weave_words": weave_words, "take_words": take_words,
            "copy_words": copy_words, "quantise_words": quantise_words, "embed": embed, "gain": gain,
            "store_embed": store_embed,
        }
        with tc.manual_schedule():
            for step in ORDER.split(","):
                words = step.split()
                name = words[0].split("@")
                numbers = [int(w) for w in words[1:]]
                if name[0] in either_engine:
                    either_engine[name[0]](*numbers, len(name) > 1)
                else:
                    one_engine[name[0]](*numbers)
